import numpy as np
import ml_dtypes


def mxq(x, axis, fmt="e4m3"):
    dtype, down = {"e4m3": (ml_dtypes.float8_e4m3fn, 7), "e5m2": (ml_dtypes.float8_e5m2, 14)}[fmt]
    v = np.moveaxis(np.asarray(x, np.float32).astype(ml_dtypes.bfloat16).astype(np.float64), axis, -1)
    blocks = v.reshape(v.shape[:-1] + (-1, 32))
    amax = np.abs(blocks).max(-1, keepdims=True)
    byte = np.maximum(np.where(amax > 0, np.frexp(amax)[1] - 1 + 127, 0) - down, 1)
    scale = np.exp2(byte - 127.0)
    codes = (blocks / scale).astype(np.float32).astype(dtype).astype(np.float64)
    return np.moveaxis((codes * scale).reshape(v.shape), -1, axis)


WIDE = False


def mx_kscale(k):
    if not WIDE:
        return np.ones(k)
    levels = np.array([10, -10, 5, -5, 0])
    if k % 512:
        return np.exp2(np.random.permutation(np.resize(levels, k // 32))).repeat(32)
    a = np.empty((k // 512, 16))
    for p in range(k // 512):
        a[p, :8] = np.random.permutation(np.resize(levels, 8))
        for g in range(8):
            far = levels[np.abs(levels - a[p, g]) >= 10]
            a[p, g + 8] = far[np.random.randint(len(far))]
    return np.exp2(a.ravel()).repeat(32)


def f64(x):
    return np.asarray(x).astype(np.float64)


def striped(idx):
    return np.tile(idx.reshape(-1, 16).T, (8, 1)).astype(np.uint16)


def unstriped(offs):
    return offs[:16].T.reshape(-1).astype(np.int64)


def striped8(idx):
    return np.concatenate([x.reshape(-1, 16).T for x in idx]).astype(np.uint16)


def runs(offs, k):
    lists = np.stack([offs[16 * r : 16 * r + 16].T.reshape(-1) for r in range(8)]).astype(np.int64)
    return lists[np.arange(k) % 512 // 64]


def pack_weight(w):
    k, n = w.shape
    w = f64(np.asarray(w, np.float32).astype(ml_dtypes.bfloat16)).reshape(k // 32, 32, n)
    amax = np.abs(w).max(1)
    byte = np.clip(np.where(amax > 0, np.frexp(amax)[1] - 1 + 127 - 7, 1), 1, 254)
    scaled = (w * np.exp2(127.0 - byte)[:, None, :]).reshape(k, n).astype(np.float32)
    words = np.ascontiguousarray(scaled.reshape(k // 512, 128, 4, n).transpose(0, 1, 3, 2)).astype(ml_dtypes.float8_e4m3fn).view(np.uint8)
    return words, np.ascontiguousarray(byte.astype(np.uint8).reshape(k // 512, 16, n))


def unpack_weight(words, scales):
    g, p, n, _ = words.shape
    vals = np.ascontiguousarray(words).view(ml_dtypes.float8_e4m3fn).astype(np.float64) * np.repeat(np.exp2(scales.astype(np.float64) - 127.0), 8, axis=1)[..., None]
    return vals.transpose(0, 1, 3, 2).reshape(g * 512, n)


def sigmoid(v):
    return 1.0 / (1.0 + np.exp(-np.maximum(v, -700.0)))


K, T, S, V, H = 512, 2048, 512, 512, 512


def setup_inputs():
    n = np.random.standard_normal
    s = mx_kscale(K)[:, None]
    u = mx_kscale(S)
    packed_xT = pack_weight(n((K, T)) * s)
    return {
        "x_words": packed_xT[0],
        "x_scales": packed_xT[1],
        "w1": (n((K, H)) / np.sqrt(K) / s).astype(np.float32),
        "w2": (n((K, H)) / np.sqrt(K) / s).astype(np.float32),
        "w3": (n((K, H)) / np.sqrt(K) / s).astype(np.float32),
        "ga": (np.random.uniform(0.5, 1.5, (H, 1)) * u[:, None]).astype(np.float32),
        "gb": (np.random.uniform(0.5, 1.5, (H, 1)) / u[:, None]).astype(np.float32),
        "offs": striped(np.random.permutation(T)[:S]),
        "two": striped(np.random.permutation(T)[:S]),
        "n1": striped8(np.stack([np.random.permutation(S) for _ in range(8)])),
        "n2": striped8(np.stack([np.random.permutation(S) for _ in range(8)])),
        "three": striped(np.random.permutation(T)[:V]),
        "n3": striped8(np.stack([np.random.permutation(V) for _ in range(8)])),
        "n4": striped8(np.stack([np.random.permutation(V) for _ in range(8)])),
        "n5": striped8(np.stack([np.random.permutation(V) for _ in range(8)])),
        "n6": striped8(np.stack([np.random.permutation(V) for _ in range(8)])),
    }


def reference(x_words, x_scales, w1, w2, w3, ga, gb, offs, two, n1, n2, three, n3, n4, n5, n6):
    xq = unpack_weight(x_words, x_scales)[:, unstriped(offs)]
    y = mxq(f64(w1), 0, "e4m3").T @ xq
    x_two = unpack_weight(x_words, x_scales)[:, unstriped(two)]
    d = mxq(f64(w2), 0, "e4m3").T @ x_two
    z = f64(ga) * (y * (sigmoid(d[np.arange(H)[:, None], runs(n2, H)])) - (0.5 * (y[np.arange(H)[:, None], runs(n1, H)])))
    x_three = unpack_weight(x_words, x_scales)[:, unstriped(three)]
    b = mxq(f64(w3), 0, "e4m3").T @ x_three
    z2 = f64(gb) * (np.minimum(np.maximum(b, b[np.arange(H)[:, None], runs(n3, H)]), b[np.arange(H)[:, None], runs(n4, H)]))
    s = 0.0625 * ((mxq(z, 0, "e4m3").T @ mxq(z2, 0, "e4m3")))
    return (s - (s[np.arange(S)[:, None], runs(n5, S)])) * (sigmoid(s[np.arange(S)[:, None], runs(n6, S)]))

@@ -1,0 +1,216 @@
+from contextlib import ExitStack
+
+import concourse.mybir as mybir
+
+K, T, S, H = 512, 2048, 512, 512
+FLOPS = 4 * 2 * 512 * 512 * 512
+
+F32 = mybir.dt.float32
+BF16 = mybir.dt.bfloat16
+I32 = mybir.dt.int32
+U32 = mybir.dt.uint32
+U16 = mybir.dt.uint16
+U8 = mybir.dt.uint8
+FP8X4 = mybir.dt.float8_e4m3fn_x4
+ALU = mybir.AluOpType
+ACT = mybir.ActivationFunctionType
+
+P = 128
+PACK = 4
+TILES = 4
+LINE = 4
+WINDOW = 2 * S
+
+
+def tile_picked_twkgatebminmxgdif_none_p_kernel(
+    tc, x_words, x_scales, w1, w2, w3, ga, gb, offs, two, n1, n2, three, n3, n4, n5, n6, out
+):
+    nc = tc.nc
+    with ExitStack() as ctx:
+        lists = ctx.enter_context(tc.tile_pool(name="lists", bufs=1))
+        keep = ctx.enter_context(tc.tile_pool(name="keep", bufs=1))
+        ring = ctx.enter_context(tc.tile_pool(name="ring", bufs=2))
+        psum = ctx.enter_context(tc.psum_pool(name="psum", bufs=1))
+
+        def load_list(name, src):
+            tile = lists.tile([P, S // 16], U16, name=name)
+            nc.sync.dma_start(tile[:], src)
+            return tile
+
+        def load_weight(name, src):
+            tile = keep.tile([P, PACK, H], F32, name=name)
+            nc.sync.dma_start(tile[:], src.rearrange("(p j) c -> p j c", j=PACK))
+            return tile
+
+        table_scales = keep.tile([P, T], U8, name="table_scales")
+        nc.gpsimd.memset(table_scales[:].bitcast(I32), 0)
+        warm = keep.tile([P, 2], F32, name="warm")
+        nc.gpsimd.memset(warm[:, 0:1], 0.0)
+        nc.scalar.activation(warm[:, 1:2], warm[:, 0:1], ACT.Sigmoid)
+
+        three_t = load_list("three_t", three)
+        table_words = keep.tile([P, T], I32, name="table_words")
+        nc.sync.dma_start(table_words[:], x_words[0].rearrange("p n t -> p (n t)").bitcast(I32))
+        for q in range(4):
+            nc.scalar.dma_start(
+                table_scales[32 * q : 32 * q + 4, :].bitcast(I32), x_scales[0, 4 * q : 4 * q + 4, :].bitcast(I32)
+            )
+        two_t = load_list("two_t", two)
+        offs_t = load_list("offs_t", offs)
+        w3_raw = load_weight("w3_raw", w3)
+        ga_t = keep.tile([P, TILES], F32, name="ga_t")
+        gb_t = keep.tile([P, TILES], F32, name="gb_t")
+        nc.gpsimd.dma_start(gb_t[:], gb.rearrange("(p t) o -> p (t o)", t=TILES))
+        nc.gpsimd.dma_start(ga_t[:], ga.rearrange("(p t) o -> p (t o)", t=TILES))
+        n3_t = load_list("n3_t", n3)
+        n4_t = load_list("n4_t", n4)
+        w2_raw = load_weight("w2_raw", w2)
+        w1_raw = load_weight("w1_raw", w1)
+        n1_t = load_list("n1_t", n1)
+        n2_t = load_list("n2_t", n2)
+        n5_t = load_list("n5_t", n5)
+        n6_t = load_list("n6_t", n6)
+
+        sign = keep.tile([P, TILES], F32, name="sign")
+        gb_abs = keep.tile([P, TILES], F32, name="gb_abs")
+        ga_signed = keep.tile([P, TILES], F32, name="ga_signed")
+        ga_half = keep.tile([P, TILES], F32, name="ga_half")
+        is_pos = keep.tile([P, TILES], F32, name="is_pos")
+        nc.gpsimd.tensor_scalar(is_pos[:], gb_t[:], 0.0, 2.0, ALU.is_ge, ALU.mult)
+        nc.gpsimd.tensor_scalar(sign[:], is_pos[:], 1.0, -1.0, ALU.mult, ALU.add)
+        nc.gpsimd.tensor_tensor(gb_abs[:], gb_t[:], sign[:], ALU.mult)
+        nc.gpsimd.tensor_tensor(ga_signed[:], ga_t[:], sign[:], ALU.mult)
+        nc.gpsimd.tensor_scalar(ga_half[:], ga_signed[:], -0.5, 0.0, ALU.mult, ALU.add)
+
+        def pick_scales(name, offsets, tag=None):
+            tile = keep.tile([P, S], U8, name=name, tag=tag or name, align_bytes=64)
+            nc.vector.tensor_copy(tile[:], table_scales[:].indirect(offsets[:]))
+            return tile
+
+        def pick_words(name, offsets):
+            tile = keep.tile([P, S], U32, name=name, align_bytes=64)
+            nc.vector.tensor_copy(tile[:], table_words[:].bitcast(U32).indirect(offsets[:]))
+            return tile
+
+        def group_weight(name, raw):
+            grouped = keep.tile([P, H * PACK], BF16, name=f"{name}_grouped", tag=f"{name}_grouped", align_bytes=64)
+            nc.scalar.copy(
+                grouped[:].rearrange("p (t m j) -> p m j t", t=TILES, j=PACK),
+                raw[:].rearrange("p j (m t) -> p m j t", t=TILES),
+            )
+            return grouped
+
+        def quantize(name, grouped, width):
+            codes = keep.tile([P, width], U32, name=f"{name}_codes", align_bytes=64)
+            scales = keep.tile([P, width], U8, name=f"{name}_scales", align_bytes=64)
+            nc.vector.quantize_mx(out=codes[:].bitcast(FP8X4), scales=scales[:], in_=grouped)
+            return codes, scales
+
+        def product(bank, stationary, t, moving):
+            acc = psum.tile([P, S], F32, name=bank)
+            cols = slice(P * t, P * (t + 1))
+            nc.tensor.matmul_mx(
+                out=acc[:],
+                lhsT=stationary[0][:, cols].bitcast(FP8X4),
+                lhsT_scale=stationary[1][:, cols],
+                rhs=moving[0][:].bitcast(FP8X4),
+                rhs_scale=moving[1][:],
+                start=True,
+                stop=True,
+            )
+            return acc
+
+        def to_window(name, acc, scale):
+            window = keep.tile([P, WINDOW], F32, name=name, tag=name, align_bytes=64)
+            nc.scalar.activation(window[:, :S], acc[:], ACT.Copy, scale=scale)
+            return window
+
+        x_three = (pick_words("three_words", three_t), pick_scales("three_scales", three_t))
+        x_two = (pick_words("two_words", two_t), pick_scales("two_scales", two_t))
+        w3_q = quantize("w3", group_weight("w3", w3_raw)[:], H)
+        x_offs = (pick_words("offs_words", offs_t), pick_scales("offs_scales", offs_t, "w3_grouped"))
+
+        w2_grouped = group_weight("w2", w2_raw)
+        b_win, b_round = [], []
+        for t in range(TILES):
+            acc = product(f"bank{t}", w3_q, t, x_three)
+            b_win.append(to_window(f"b_win{t}", acc, gb_abs[:, t : t + 1]))
+            rounded = keep.tile([P, S], BF16, name=f"b_round{t}")
+            nc.scalar.activation(rounded[:], acc[:], ACT.Copy, scale=gb_abs[:, t : t + 1])
+            b_round.append(rounded)
+
+        larger = keep.tile([P, TILES, S], BF16, name="larger")
+        at_n4 = keep.tile([P, TILES, S], BF16, name="at_n4")
+        y_acc, y_win, d_win, gate = [], [], [], []
+
+        def select(t, tag):
+            at_n3 = keep.tile([P, S], BF16, name=f"at_n3_{t}", tag=tag, align_bytes=64)
+            nc.vector.tensor_copy(at_n3[:], b_win[t][:].indirect(n3_t[:]))
+            nc.vector.tensor_copy(at_n4[:, t, :], b_win[t][:].indirect(n4_t[:]))
+            nc.vector.tensor_tensor(larger[:, t, :], b_round[t][:], at_n3[:], ALU.max)
+
+        w2_q = quantize("w2", w2_grouped[:], H)
+        select(0, "at_n3_0")
+        w1_grouped = group_weight("w1", w1_raw)
+        select(1, "w2_grouped")
+        for t in range(TILES):
+            d_win.append(to_window(f"d_win{t}", product(f"bank{TILES + t}", w2_q, t, x_two), 1.0))
+        select(2, "at_n3_2")
+        w1_q = quantize("w1", w1_grouped[:], H)
+        for t in range(TILES):
+            y_acc.append(product(f"bank{TILES + t}", w1_q, t, x_offs))
+            y_win.append(to_window(f"y_win{t}", y_acc[t], ga_half[:, t : t + 1]))
+        select(3, "w1_grouped")
+        for t in range(TILES):
+            g = keep.tile([P, S], F32, name=f"gate{t}")
+            nc.scalar.activation(g[:], d_win[t][:].indirect(n2_t[:]), ACT.Sigmoid)
+            gate.append(g)
+
+        z2_planes = keep.tile([P, TILES, S], BF16, name="z2_planes")
+        nc.vector.tensor_tensor(z2_planes[:], larger[:], at_n4[:], ALU.min)
+        z2_grouped = keep.tile([P, S * PACK], BF16, name="z2_grouped", tag=f"d_win{TILES - 1}", align_bytes=64)
+        nc.scalar.copy(
+            z2_grouped[:].rearrange("p (c i t) -> p c t i", i=LINE, t=PACK),
+            z2_planes[:].rearrange("p t (c i) -> p c t i", i=LINE),
+        )
+        at_n1 = keep.tile([P, TILES, S], F32, name="at_n1")
+        gated = keep.tile([P, TILES, S], F32, name="gated")
+        for t in range(TILES):
+            nc.vector.tensor_copy(at_n1[:, t, :], y_win[t][:].indirect(n1_t[:]))
+            nc.vector.scalar_tensor_tensor(
+                gated[:, t, :], y_acc[t][:], ga_signed[:, t : t + 1], gate[t][:], ALU.mult, ALU.mult
+            )
+
+        z2 = quantize("z2", z2_grouped[:], S)
+        z_grouped = []
+        s_acc, s_win = [], []
+
+        def score(u):
+            zq = quantize(f"z_{u}", z_grouped[u][:], P)
+            s_acc.append(product(f"bank{u}", zq, 0, z2))
+            s_win.append(to_window(f"s_win{u}", s_acc[u], 0.0625))
+
+        for u in range(TILES):
+            zg = keep.tile([P, P * PACK], BF16, name=f"z_grouped{u}", align_bytes=64)
+            nc.vector.tensor_tensor(
+                zg[:].rearrange("p (q i t) -> p q t i", i=LINE, t=PACK),
+                gated[:].rearrange("p t (q u i) -> p u q t i", u=TILES, i=LINE)[:, u],
+                at_n1[:].rearrange("p t (q u i) -> p u q t i", u=TILES, i=LINE)[:, u],
+                ALU.add,
+            )
+            z_grouped.append(zg)
+            if u > 0:
+                score(u - 1)
+        score(TILES - 1)
+
+        out_rows = out.rearrange("(q u i) v -> u q i v", u=TILES, i=LINE)
+        for u in range(TILES):
+            s_gate = ring.tile([P, S], F32, name="s_gate")
+            nc.scalar.activation(s_gate[:], s_win[u][:].indirect(n6_t[:]), ACT.Sigmoid)
+            at_n5 = ring.tile([P, S], F32, name="at_n5")
+            nc.vector.tensor_copy(at_n5[:], s_win[u][:].indirect(n5_t[:]))
+            diff = ring.tile([P, S], F32, name="diff")
+            nc.vector.scalar_tensor_tensor(diff[:], s_acc[u][:], 0.0625, at_n5[:], ALU.mult, ALU.subtract)
+            result = keep.tile([P, S], F32, name=f"result{u}")
+            nc.vector.tensor_tensor(result[:], diff[:], s_gate[:], ALU.mult)
+            nc.sync.dma_start(out_rows[u], result[:])

@@ -20,6 +20,7 @@ PACK = 4
 TILES = 4
 LINE = 4
 WINDOW = 2 * S
+ROUNDED = 2
 
 
 def tile_picked_twkgatebminmxgdif_none_p_kernel(
@@ -38,7 +39,7 @@ def tile_picked_twkgatebminmxgdif_none_p_kernel(
             return tile
 
         def load_weight(name, src):
-            tile = keep.tile([P, PACK, H], F32, name=name)
+            tile = keep.tile([P, PACK, H], F32, name=name, tag=name, align_bytes=64)
             nc.sync.dma_start(tile[:], src.rearrange("(p j) c -> p j c", j=PACK))
             return tile
 
@@ -62,9 +63,9 @@ def tile_picked_twkgatebminmxgdif_none_p_kernel(
         gb_t = keep.tile([P, TILES], F32, name="gb_t")
         nc.gpsimd.dma_start(gb_t[:], gb.rearrange("(p t) o -> p (t o)", t=TILES))
         nc.gpsimd.dma_start(ga_t[:], ga.rearrange("(p t) o -> p (t o)", t=TILES))
+        w2_raw = load_weight("w2_raw", w2)
         n3_t = load_list("n3_t", n3)
         n4_t = load_list("n4_t", n4)
-        w2_raw = load_weight("w2_raw", w2)
         w1_raw = load_weight("w1_raw", w1)
         n1_t = load_list("n1_t", n1)
         n2_t = load_list("n2_t", n2)
@@ -74,13 +75,11 @@ def tile_picked_twkgatebminmxgdif_none_p_kernel(
         sign = keep.tile([P, TILES], F32, name="sign")
         gb_abs = keep.tile([P, TILES], F32, name="gb_abs")
         ga_signed = keep.tile([P, TILES], F32, name="ga_signed")
-        ga_half = keep.tile([P, TILES], F32, name="ga_half")
         is_pos = keep.tile([P, TILES], F32, name="is_pos")
         nc.gpsimd.tensor_scalar(is_pos[:], gb_t[:], 0.0, 2.0, ALU.is_ge, ALU.mult)
         nc.gpsimd.tensor_scalar(sign[:], is_pos[:], 1.0, -1.0, ALU.mult, ALU.add)
         nc.gpsimd.tensor_tensor(gb_abs[:], gb_t[:], sign[:], ALU.mult)
         nc.gpsimd.tensor_tensor(ga_signed[:], ga_t[:], sign[:], ALU.mult)
-        nc.gpsimd.tensor_scalar(ga_half[:], ga_signed[:], -0.5, 0.0, ALU.mult, ALU.add)
 
         def pick_scales(name, offsets, tag=None):
             tile = keep.tile([P, S], U8, name=name, tag=tag or name, align_bytes=64)
@@ -120,8 +119,8 @@ def tile_picked_twkgatebminmxgdif_none_p_kernel(
             )
             return acc
 
-        def to_window(name, acc, scale):
-            window = keep.tile([P, WINDOW], F32, name=name, tag=name, align_bytes=64)
+        def to_window(name, acc, scale, tag=None):
+            window = keep.tile([P, WINDOW], F32, name=name, tag=tag or name, align_bytes=64)
             nc.scalar.activation(window[:, :S], acc[:], ACT.Copy, scale=scale)
             return window
 
@@ -131,55 +130,63 @@ def tile_picked_twkgatebminmxgdif_none_p_kernel(
         x_offs = (pick_words("offs_words", offs_t), pick_scales("offs_scales", offs_t, "w3_grouped"))
 
         w2_grouped = group_weight("w2", w2_raw)
-        b_win, b_round = [], []
+        b_acc, b_win, b_round = [], [], []
         for t in range(TILES):
-            acc = product(f"bank{t}", w3_q, t, x_three)
-            b_win.append(to_window(f"b_win{t}", acc, gb_abs[:, t : t + 1]))
-            rounded = keep.tile([P, S], BF16, name=f"b_round{t}")
-            nc.scalar.activation(rounded[:], acc[:], ACT.Copy, scale=gb_abs[:, t : t + 1])
-            b_round.append(rounded)
+            b_acc.append(product(f"bank{t}", w3_q, t, x_three))
+            b_win.append(to_window(f"b_win{t}", b_acc[t], gb_abs[:, t : t + 1], "w2_raw" if t == 0 else None))
+            if t < ROUNDED:
+                rounded = keep.tile([P, S], BF16, name=f"b_round{t}")
+                nc.scalar.activation(rounded[:], b_acc[t][:], ACT.Copy, scale=gb_abs[:, t : t + 1])
+                b_round.append(rounded)
 
-        larger = keep.tile([P, TILES, S], BF16, name="larger")
-        at_n4 = keep.tile([P, TILES, S], BF16, name="at_n4")
-        y_acc, y_win, d_win, gate = [], [], [], []
+        gated = keep.tile([P, TILES * S], F32, name="gated")
+        larger = gated[:, 2 * S :].bitcast(BF16).rearrange("p (r h c) -> p h r c", r=2, h=2)
+        z2_planes = keep.tile([P, TILES, S], BF16, name="z2_planes")
+        y_win, d_win, gate = [], [], []
 
-        def select(t, tag):
-            at_n3 = keep.tile([P, S], BF16, name=f"at_n3_{t}", tag=tag, align_bytes=64)
-            nc.vector.tensor_copy(at_n3[:], b_win[t][:].indirect(n3_t[:]))
-            nc.vector.tensor_copy(at_n4[:, t, :], b_win[t][:].indirect(n4_t[:]))
-            nc.vector.tensor_tensor(larger[:, t, :], b_round[t][:], at_n3[:], ALU.max)
+        def select_pair(first, tag):
+            fetched = keep.tile([P, 2, 2, S], BF16, name=f"fetched{first}", tag=tag, align_bytes=64)
+            for t in (first, first + 1):
+                at_n3 = fetched[:, 0, t - first, :]
+                nc.vector.tensor_copy(at_n3, b_win[t][:].indirect(n3_t[:]))
+                nc.vector.tensor_copy(fetched[:, 1, t - first, :], b_win[t][:].indirect(n4_t[:]))
+                if t < ROUNDED:
+                    nc.vector.tensor_tensor(larger[:, t // 2, t % 2, :], b_round[t][:], at_n3, ALU.max)
+                else:
+                    nc.vector.scalar_tensor_tensor(
+                        larger[:, t // 2, t % 2, :], b_acc[t][:], gb_abs[:, t : t + 1], at_n3, ALU.mult, ALU.max
+                    )
+            return fetched
+
+        def smaller(first, fetched):
+            pair = slice(first, first + 2)
+            nc.vector.tensor_tensor(z2_planes[:, pair, :], larger[:, first // 2], fetched[:, 1], ALU.min)
 
         w2_q = quantize("w2", w2_grouped[:], H)
-        select(0, "at_n3_0")
+        fetched_low = select_pair(0, "w2_grouped")
         w1_grouped = group_weight("w1", w1_raw)
-        select(1, "w2_grouped")
         for t in range(TILES):
-            d_win.append(to_window(f"d_win{t}", product(f"bank{TILES + t}", w2_q, t, x_two), 1.0))
-        select(2, "at_n3_2")
+            d_win.append(to_window(f"d_win{t}", product(f"bank{TILES + t}", w2_q, t, x_two), 1.0, "w1_raw" if t == 0 else None))
         w1_q = quantize("w1", w1_grouped[:], H)
+        smaller(0, fetched_low)
+        fetched_high = select_pair(2, "w1_grouped")
         for t in range(TILES):
-            y_acc.append(product(f"bank{TILES + t}", w1_q, t, x_offs))
-            y_win.append(to_window(f"y_win{t}", y_acc[t], ga_half[:, t : t + 1]))
-        select(3, "w1_grouped")
+            y_win.append(to_window(f"y_win{t}", product(f"bank{TILES + t}", w1_q, t, x_offs), ga_signed[:, t : t + 1]))
         for t in range(TILES):
             g = keep.tile([P, S], F32, name=f"gate{t}")
             nc.scalar.activation(g[:], d_win[t][:].indirect(n2_t[:]), ACT.Sigmoid)
             gate.append(g)
 
-        z2_planes = keep.tile([P, TILES, S], BF16, name="z2_planes")
-        nc.vector.tensor_tensor(z2_planes[:], larger[:], at_n4[:], ALU.min)
+        smaller(2, fetched_high)
         z2_grouped = keep.tile([P, S * PACK], BF16, name="z2_grouped", tag=f"d_win{TILES - 1}", align_bytes=64)
         nc.scalar.copy(
             z2_grouped[:].rearrange("p (c i t) -> p c t i", i=LINE, t=PACK),
             z2_planes[:].rearrange("p t (c i) -> p c t i", i=LINE),
         )
         at_n1 = keep.tile([P, TILES, S], F32, name="at_n1")
-        gated = keep.tile([P, TILES, S], F32, name="gated")
         for t in range(TILES):
-            nc.vector.tensor_copy(at_n1[:, t, :], y_win[t][:].indirect(n1_t[:]))
-            nc.vector.scalar_tensor_tensor(
-                gated[:, t, :], y_acc[t][:], ga_signed[:, t : t + 1], gate[t][:], ALU.mult, ALU.mult
-            )
+            nc.vector.tensor_scalar(at_n1[:, t, :], y_win[t][:].indirect(n1_t[:]), -0.5, 0.0, ALU.mult, ALU.add)
+            nc.gpsimd.tensor_tensor(gated[:, S * t : S * (t + 1)], y_win[t][:, :S], gate[t][:], ALU.mult)
 
         z2 = quantize("z2", z2_grouped[:], S)
         z_grouped = []
@@ -194,7 +201,7 @@ def tile_picked_twkgatebminmxgdif_none_p_kernel(
             zg = keep.tile([P, P * PACK], BF16, name=f"z_grouped{u}", align_bytes=64)
             nc.vector.tensor_tensor(
                 zg[:].rearrange("p (q i t) -> p q t i", i=LINE, t=PACK),
-                gated[:].rearrange("p t (q u i) -> p u q t i", u=TILES, i=LINE)[:, u],
+                gated[:].rearrange("p (t q u i) -> p u q t i", t=TILES, u=TILES, i=LINE)[:, u],
                 at_n1[:].rearrange("p t (q u i) -> p u q t i", u=TILES, i=LINE)[:, u],
                 ALU.add,
             )
@@ -204,13 +211,42 @@ def tile_picked_twkgatebminmxgdif_none_p_kernel(
         score(TILES - 1)
 
         out_rows = out.rearrange("(q u i) v -> u q i v", u=TILES, i=LINE)
-        for u in range(TILES):
-            s_gate = ring.tile([P, S], F32, name="s_gate")
-            nc.scalar.activation(s_gate[:], s_win[u][:].indirect(n6_t[:]), ACT.Sigmoid)
-            at_n5 = ring.tile([P, S], F32, name="at_n5")
-            nc.vector.tensor_copy(at_n5[:], s_win[u][:].indirect(n5_t[:]))
-            diff = ring.tile([P, S], F32, name="diff")
-            nc.vector.scalar_tensor_tensor(diff[:], s_acc[u][:], 0.0625, at_n5[:], ALU.mult, ALU.subtract)
+        s_gate, at_n5 = [], []
+
+        def fetch(u):
+            s_gate.append(keep.tile([P, S], F32, name=f"s_gate{u}"))
+            nc.scalar.activation(s_gate[u][:], s_win[u][:].indirect(n6_t[:]), ACT.Sigmoid)
+            at_n5.append(ring.tile([P, S], F32, name="at_n5"))
+            nc.vector.tensor_copy(at_n5[u][:], s_win[u][:].indirect(n5_t[:]))
+
+        def finish(u, engine):
+            diff = keep.tile([P, S], F32, name=f"diff{u}")
+            nc.vector.scalar_tensor_tensor(diff[:], s_acc[u][:], 0.0625, at_n5[u][:], ALU.mult, ALU.subtract)
             result = keep.tile([P, S], F32, name=f"result{u}")
-            nc.vector.tensor_tensor(result[:], diff[:], s_gate[:], ALU.mult)
+            engine.tensor_tensor(result[:], diff[:], s_gate[u][:], ALU.mult)
             nc.sync.dma_start(out_rows[u], result[:])
+
+        fetch(0)
+        fetch(1)
+        finish(0, nc.gpsimd)
+        fetch(2)
+        finish(1, nc.gpsimd)
+        finish(2, nc.gpsimd)
+
+        last = TILES - 1
+        halves = [slice(0, S // 2), slice(S // 2, S)]
+        last_gate = keep.tile([P, S], F32, name="last_gate")
+        nc.scalar.activation(last_gate[:], s_win[last][:].indirect(n6_t[:]), ACT.Sigmoid)
+        last_n5 = ring.tile([P, S], F32, name="at_n5")
+        last_diff = keep.tile([P, S], F32, name="last_diff")
+        last_result = keep.tile([P, S], F32, name="last_result")
+        for cols in halves:
+            offsets = n5_t[:, cols.start // 16 : cols.stop // 16]
+            nc.vector.tensor_copy(last_n5[:, cols], s_win[last][:].indirect(offsets))
+        for cols in halves:
+            nc.vector.scalar_tensor_tensor(
+                last_diff[:, cols], s_acc[last][:, cols], 0.0625, last_n5[:, cols], ALU.mult, ALU.subtract
+            )
+        for cols in halves:
+            nc.vector.tensor_tensor(last_result[:, cols], last_diff[:, cols], last_gate[:, cols], ALU.mult)
+            nc.sync.dma_start(out_rows[last][:, :, cols], last_result[:, cols])

from contextlib import ExitStack

import concourse.mybir as mybir

K, T, S, H = 512, 2048, 512, 512
FLOPS = 4 * 2 * 512 * 512 * 512

F32 = mybir.dt.float32
BF16 = mybir.dt.bfloat16
I32 = mybir.dt.int32
U32 = mybir.dt.uint32
U16 = mybir.dt.uint16
U8 = mybir.dt.uint8
FP8X4 = mybir.dt.float8_e4m3fn_x4
ALU = mybir.AluOpType
ACT = mybir.ActivationFunctionType

P = 128
PACK = 4
TILES = 4
LINE = 4
WINDOW = 2 * S
ROUNDED = 2


def tile_picked_twkgatebminmxgdif_none_p_kernel(
    tc, x_words, x_scales, w1, w2, w3, ga, gb, offs, two, n1, n2, three, n3, n4, n5, n6, out
):
    nc = tc.nc
    with ExitStack() as ctx:
        lists = ctx.enter_context(tc.tile_pool(name="lists", bufs=1))
        keep = ctx.enter_context(tc.tile_pool(name="keep", bufs=1))
        ring = ctx.enter_context(tc.tile_pool(name="ring", bufs=2))
        psum = ctx.enter_context(tc.psum_pool(name="psum", bufs=1))

        def load_list(name, src):
            tile = lists.tile([P, S // 16], U16, name=name)
            nc.sync.dma_start(tile[:], src)
            return tile

        def load_weight(name, src):
            tile = keep.tile([P, PACK, H], F32, name=name, tag=name, align_bytes=64)
            nc.sync.dma_start(tile[:], src.rearrange("(p j) c -> p j c", j=PACK))
            return tile

        table_scales = keep.tile([P, T], U8, name="table_scales")
        nc.gpsimd.memset(table_scales[:].bitcast(I32), 0)
        warm = keep.tile([P, 2], F32, name="warm")
        nc.gpsimd.memset(warm[:, 0:1], 0.0)
        nc.scalar.activation(warm[:, 1:2], warm[:, 0:1], ACT.Sigmoid)

        three_t = load_list("three_t", three)
        table_words = keep.tile([P, T], I32, name="table_words")
        nc.sync.dma_start(table_words[:], x_words[0].rearrange("p n t -> p (n t)").bitcast(I32))
        for q in range(4):
            nc.scalar.dma_start(
                table_scales[32 * q : 32 * q + 4, :].bitcast(I32), x_scales[0, 4 * q : 4 * q + 4, :].bitcast(I32)
            )
        two_t = load_list("two_t", two)
        offs_t = load_list("offs_t", offs)
        w3_raw = load_weight("w3_raw", w3)
        ga_t = keep.tile([P, TILES], F32, name="ga_t")
        gb_t = keep.tile([P, TILES], F32, name="gb_t")
        nc.gpsimd.dma_start(gb_t[:], gb.rearrange("(p t) o -> p (t o)", t=TILES))
        nc.gpsimd.dma_start(ga_t[:], ga.rearrange("(p t) o -> p (t o)", t=TILES))
        w2_raw = load_weight("w2_raw", w2)
        n3_t = load_list("n3_t", n3)
        n4_t = load_list("n4_t", n4)
        w1_raw = load_weight("w1_raw", w1)
        n1_t = load_list("n1_t", n1)
        n2_t = load_list("n2_t", n2)
        n5_t = load_list("n5_t", n5)
        n6_t = load_list("n6_t", n6)

        sign = keep.tile([P, TILES], F32, name="sign")
        gb_abs = keep.tile([P, TILES], F32, name="gb_abs")
        ga_signed = keep.tile([P, TILES], F32, name="ga_signed")
        is_pos = keep.tile([P, TILES], F32, name="is_pos")
        nc.gpsimd.tensor_scalar(is_pos[:], gb_t[:], 0.0, 2.0, ALU.is_ge, ALU.mult)
        nc.gpsimd.tensor_scalar(sign[:], is_pos[:], 1.0, -1.0, ALU.mult, ALU.add)
        nc.gpsimd.tensor_tensor(gb_abs[:], gb_t[:], sign[:], ALU.mult)
        nc.gpsimd.tensor_tensor(ga_signed[:], ga_t[:], sign[:], ALU.mult)

        def pick_scales(name, offsets, tag=None):
            tile = keep.tile([P, S], U8, name=name, tag=tag or name, align_bytes=64)
            nc.vector.tensor_copy(tile[:], table_scales[:].indirect(offsets[:]))
            return tile

        def pick_words(name, offsets):
            tile = keep.tile([P, S], U32, name=name, align_bytes=64)
            nc.vector.tensor_copy(tile[:], table_words[:].bitcast(U32).indirect(offsets[:]))
            return tile

        def group_weight(name, raw):
            grouped = keep.tile([P, H * PACK], BF16, name=f"{name}_grouped", tag=f"{name}_grouped", align_bytes=64)
            nc.scalar.copy(
                grouped[:].rearrange("p (t m j) -> p m j t", t=TILES, j=PACK),
                raw[:].rearrange("p j (m t) -> p m j t", t=TILES),
            )
            return grouped

        def quantize(name, grouped, width):
            codes = keep.tile([P, width], U32, name=f"{name}_codes", align_bytes=64)
            scales = keep.tile([P, width], U8, name=f"{name}_scales", align_bytes=64)
            nc.vector.quantize_mx(out=codes[:].bitcast(FP8X4), scales=scales[:], in_=grouped)
            return codes, scales

        def product(bank, stationary, t, moving):
            acc = psum.tile([P, S], F32, name=bank)
            cols = slice(P * t, P * (t + 1))
            nc.tensor.matmul_mx(
                out=acc[:],
                lhsT=stationary[0][:, cols].bitcast(FP8X4),
                lhsT_scale=stationary[1][:, cols],
                rhs=moving[0][:].bitcast(FP8X4),
                rhs_scale=moving[1][:],
                start=True,
                stop=True,
            )
            return acc

        def to_window(name, acc, scale, tag=None):
            window = keep.tile([P, WINDOW], F32, name=name, tag=tag or name, align_bytes=64)
            nc.scalar.activation(window[:, :S], acc[:], ACT.Copy, scale=scale)
            return window

        x_three = (pick_words("three_words", three_t), pick_scales("three_scales", three_t))
        x_two = (pick_words("two_words", two_t), pick_scales("two_scales", two_t))
        w3_q = quantize("w3", group_weight("w3", w3_raw)[:], H)
        x_offs = (pick_words("offs_words", offs_t), pick_scales("offs_scales", offs_t, "w3_grouped"))

        w2_grouped = group_weight("w2", w2_raw)
        b_acc, b_win, b_round = [], [], []
        for t in range(TILES):
            b_acc.append(product(f"bank{t}", w3_q, t, x_three))
            b_win.append(to_window(f"b_win{t}", b_acc[t], gb_abs[:, t : t + 1], "w2_raw" if t == 0 else None))
            if t < ROUNDED:
                rounded = keep.tile([P, S], BF16, name=f"b_round{t}")
                nc.scalar.activation(rounded[:], b_acc[t][:], ACT.Copy, scale=gb_abs[:, t : t + 1])
                b_round.append(rounded)

        gated = keep.tile([P, TILES * S], F32, name="gated")
        larger = gated[:, 2 * S :].bitcast(BF16).rearrange("p (r h c) -> p h r c", r=2, h=2)
        z2_planes = keep.tile([P, TILES, S], BF16, name="z2_planes")
        y_win, d_win, gate = [], [], []

        def select_pair(first, tag):
            fetched = keep.tile([P, 2, 2, S], BF16, name=f"fetched{first}", tag=tag, align_bytes=64)
            for t in (first, first + 1):
                at_n3 = fetched[:, 0, t - first, :]
                nc.vector.tensor_copy(at_n3, b_win[t][:].indirect(n3_t[:]))
                nc.vector.tensor_copy(fetched[:, 1, t - first, :], b_win[t][:].indirect(n4_t[:]))
                if t < ROUNDED:
                    nc.vector.tensor_tensor(larger[:, t // 2, t % 2, :], b_round[t][:], at_n3, ALU.max)
                else:
                    nc.vector.scalar_tensor_tensor(
                        larger[:, t // 2, t % 2, :], b_acc[t][:], gb_abs[:, t : t + 1], at_n3, ALU.mult, ALU.max
                    )
            return fetched

        def smaller(first, fetched):
            pair = slice(first, first + 2)
            nc.vector.tensor_tensor(z2_planes[:, pair, :], larger[:, first // 2], fetched[:, 1], ALU.min)

        w2_q = quantize("w2", w2_grouped[:], H)
        fetched_low = select_pair(0, "w2_grouped")
        w1_grouped = group_weight("w1", w1_raw)
        for t in range(TILES):
            d_win.append(to_window(f"d_win{t}", product(f"bank{TILES + t}", w2_q, t, x_two), 1.0, "w1_raw" if t == 0 else None))
        w1_q = quantize("w1", w1_grouped[:], H)
        smaller(0, fetched_low)
        fetched_high = select_pair(2, "w1_grouped")
        for t in range(TILES):
            y_win.append(to_window(f"y_win{t}", product(f"bank{TILES + t}", w1_q, t, x_offs), ga_signed[:, t : t + 1]))
        for t in range(TILES):
            g = keep.tile([P, S], F32, name=f"gate{t}")
            nc.scalar.activation(g[:], d_win[t][:].indirect(n2_t[:]), ACT.Sigmoid)
            gate.append(g)

        smaller(2, fetched_high)
        z2_grouped = keep.tile([P, S * PACK], BF16, name="z2_grouped", tag=f"d_win{TILES - 1}", align_bytes=64)
        nc.scalar.copy(
            z2_grouped[:].rearrange("p (c i t) -> p c t i", i=LINE, t=PACK),
            z2_planes[:].rearrange("p t (c i) -> p c t i", i=LINE),
        )
        at_n1 = keep.tile([P, TILES, S], F32, name="at_n1")
        for t in range(TILES):
            nc.vector.tensor_scalar(at_n1[:, t, :], y_win[t][:].indirect(n1_t[:]), -0.5, 0.0, ALU.mult, ALU.add)
            nc.gpsimd.tensor_tensor(gated[:, S * t : S * (t + 1)], y_win[t][:, :S], gate[t][:], ALU.mult)

        z2 = quantize("z2", z2_grouped[:], S)
        z_grouped = []
        s_acc, s_win = [], []

        def score(u):
            zq = quantize(f"z_{u}", z_grouped[u][:], P)
            s_acc.append(product(f"bank{u}", zq, 0, z2))
            s_win.append(to_window(f"s_win{u}", s_acc[u], 0.0625))

        for u in range(TILES):
            zg = keep.tile([P, P * PACK], BF16, name=f"z_grouped{u}", align_bytes=64)
            nc.vector.tensor_tensor(
                zg[:].rearrange("p (q i t) -> p q t i", i=LINE, t=PACK),
                gated[:].rearrange("p (t q u i) -> p u q t i", t=TILES, u=TILES, i=LINE)[:, u],
                at_n1[:].rearrange("p t (q u i) -> p u q t i", u=TILES, i=LINE)[:, u],
                ALU.add,
            )
            z_grouped.append(zg)
            if u > 0:
                score(u - 1)
        score(TILES - 1)

        out_rows = out.rearrange("(q u i) v -> u q i v", u=TILES, i=LINE)
        s_gate, at_n5 = [], []

        def fetch(u):
            s_gate.append(keep.tile([P, S], F32, name=f"s_gate{u}"))
            nc.scalar.activation(s_gate[u][:], s_win[u][:].indirect(n6_t[:]), ACT.Sigmoid)
            at_n5.append(ring.tile([P, S], F32, name="at_n5"))
            nc.vector.tensor_copy(at_n5[u][:], s_win[u][:].indirect(n5_t[:]))

        def finish(u, engine):
            diff = keep.tile([P, S], F32, name=f"diff{u}")
            nc.vector.scalar_tensor_tensor(diff[:], s_acc[u][:], 0.0625, at_n5[u][:], ALU.mult, ALU.subtract)
            result = keep.tile([P, S], F32, name=f"result{u}")
            engine.tensor_tensor(result[:], diff[:], s_gate[u][:], ALU.mult)
            nc.sync.dma_start(out_rows[u], result[:])

        fetch(0)
        fetch(1)
        finish(0, nc.gpsimd)
        fetch(2)
        finish(1, nc.gpsimd)
        finish(2, nc.gpsimd)

        last = TILES - 1
        halves = [slice(0, S // 2), slice(S // 2, S)]
        last_gate = keep.tile([P, S], F32, name="last_gate")
        nc.scalar.activation(last_gate[:], s_win[last][:].indirect(n6_t[:]), ACT.Sigmoid)
        last_n5 = ring.tile([P, S], F32, name="at_n5")
        last_diff = keep.tile([P, S], F32, name="last_diff")
        last_result = keep.tile([P, S], F32, name="last_result")
        for cols in halves:
            offsets = n5_t[:, cols.start // 16 : cols.stop // 16]
            nc.vector.tensor_copy(last_n5[:, cols], s_win[last][:].indirect(offsets))
        for cols in halves:
            nc.vector.scalar_tensor_tensor(
                last_diff[:, cols], s_acc[last][:, cols], 0.0625, last_n5[:, cols], ALU.mult, ALU.subtract
            )
        for cols in halves:
            nc.vector.tensor_tensor(last_result[:, cols], last_diff[:, cols], last_gate[:, cols], ALU.mult)
            nc.sync.dma_start(out_rows[last][:, :, cols], last_result[:, cols])
